import numpy as np
import ml_dtypes


def mxq(x, axis, fmt="e4m3"):
    dtype, down = {"e4m3": (ml_dtypes.float8_e4m3fn, 7), "e5m2": (ml_dtypes.float8_e5m2, 14)}[fmt]
    v = np.moveaxis(np.asarray(x, np.float32).astype(ml_dtypes.bfloat16).astype(np.float64), axis, -1)
    blocks = v.reshape(v.shape[:-1] + (-1, 32))
    amax = np.abs(blocks).max(-1, keepdims=True)
    byte = np.maximum(np.where(amax > 0, np.frexp(amax)[1] - 1 + 127, 0) - down, 1)
    scale = np.exp2(byte - 127.0)
    codes = (blocks / scale).astype(np.float32).astype(dtype).astype(np.float64)
    return np.moveaxis((codes * scale).reshape(v.shape), -1, axis)


WIDE = False


def mx_kscale(k):
    if not WIDE:
        return np.ones(k)
    levels = np.array([10, -10, 5, -5, 0])
    if k % 512:
        return np.exp2(np.random.permutation(np.resize(levels, k // 32))).repeat(32)
    a = np.empty((k // 512, 16))
    for p in range(k // 512):
        a[p, :8] = np.random.permutation(np.resize(levels, 8))
        for g in range(8):
            far = levels[np.abs(levels - a[p, g]) >= 10]
            a[p, g + 8] = far[np.random.randint(len(far))]
    return np.exp2(a.ravel()).repeat(32)


BF16 = ml_dtypes.bfloat16


def bf(x):
    return np.asarray(x, np.float32).astype(BF16)


def f64(x):
    return np.asarray(x).astype(np.float64)

def planes(Y):
    n, m = Y.shape
    b = f64(bf(Y)).reshape(n // 32, 32, m)
    amax = np.abs(b).max(1)
    byte = np.clip(np.where(amax > 0, np.frexp(amax)[1] - 1 + 127 - 7, 1), 1, 254)
    codes = (b * np.exp2(127.0 - byte)[:, None, :]).reshape(n, m).astype(np.float32).astype(ml_dtypes.float8_e4m3fn).view(np.uint8)
    words = codes.reshape(n // 512, 128, 4, m).transpose(0, 1, 3, 2)
    return np.ascontiguousarray(words), np.ascontiguousarray(byte.astype(np.uint8).reshape(n // 512, 16, m))


H, C, D, E, N0, N1, N2, L = 2, 512, 512, 512, 2048, 1024, 512, 3
P = N0 + N1 + N2


def softplus(a):
    return np.log(1.0 + np.exp(a))


def bucket_state(k_b, vh_b, n):
    s = mxq(k_b, 1, "e4m3").transpose(0, 2, 1) @ mxq(vh_b, 1, "e4m3")
    return s / np.sqrt(n)


def bucket_read(qq, s):
    r = qq @ mxq(s, 1, "e4m3")
    return r / np.sqrt(qq.shape[-1])


def setup_inputs():
    s, t = mx_kscale(P), mx_kscale(D)
    return {"q": bf(np.random.standard_normal((H, C, D)) * t),
            "k": bf(np.random.standard_normal((H, P, D)) * s[:, None] / t),
            "v": bf(np.random.standard_normal((H, P, E)) / s[:, None]),
            "wdec": bf(np.random.uniform(0.5, 1.5, (H, P))),
            "lam": bf(np.random.standard_normal((H, C, L)))}


def core(q, k, v, wdec, lam):
    q, k, v, wdec, lam = f64(q), f64(k), f64(v), f64(wdec), f64(lam)
    vh = wdec[:, :, None] * v
    g = softplus(lam)
    qq = mxq(q, 2, "e4m3")
    o = np.zeros((q.shape[0], q.shape[1], v.shape[2]))
    start = 0
    for l, n in enumerate((N0, N1, N2)):
        stop = start + n
        s_l = bucket_state(k[:, start:stop, :], vh[:, start:stop, :], n)
        r_l = bucket_read(qq, s_l)
        o = o + g[:, :, l][:, :, None] * r_l
        start = stop
    return o


def reference(q, k, v, wdec, lam):
    R_out = core(q, k, v, wdec, lam)
    words, scales = planes(np.moveaxis(R_out, 2, 0).reshape(512, -1))
    return R_out, words, scales

@@ -1,0 +1,476 @@
+from contextlib import ExitStack
+
+import concourse.mybir as mybir
+from concourse.masks import make_identity
+
+F32 = mybir.dt.float32
+BF16 = mybir.dt.bfloat16
+U32 = mybir.dt.uint32
+I32 = mybir.dt.int32
+U8 = mybir.dt.uint8
+FP8X4 = mybir.dt.float8_e4m3fn_x4
+ALU = mybir.AluOpType
+ACT = mybir.ActivationFunctionType
+
+P = 128
+PACK = 4
+PASS = P * PACK
+H, C, D, E = 2, 512, 512, 512
+LENS = (2048, 1024, 512)
+STARTS = (0, 2048, 3072)
+PAST = sum(LENS)
+TT = C // P
+FLOPS = 2 * H * (PAST * D * E + 3 * C * D * E)
+
+AHEAD = 8
+BUCKETS = ((0, 2), (0, 1), (1, 0), (0, 0), (1, 1), (1, 2))
+JOBS = (
+    ("lv", 0,),
+    ("lk", 0,),
+    ("lv", 1,),
+    ("lk", 1,),
+    ("lv", 2,),
+    ("lk", 2,),
+    ("lv", 3,),
+    ("lk", 3,),
+    ("lq", 0,),
+    ("lv", 4,),
+    ("lk", 4,),
+    ("lv", 5,),
+    ("lk", 5,),
+    ("lv", 6,),
+    ("lk", 6,),
+    ("lv", 7,),
+    ("lk", 7,),
+    ("ga",),
+    ("lq", 1,),
+    ("mult", 0,),
+    ("KI", 0,),
+    ("mult", 1,),
+    ("qk", 0,),
+    ("VI", 0,),
+    ("lv", 8,),
+    ("lk", 8,),
+    ("VI", 1,),
+    ("KI", 1,),
+    ("mult", 2,),
+    ("qv", 0,),
+    ("qk", 1,),
+    ("lv", 9,),
+    ("lk", 9,),
+    ("smm", 0, 0,),
+    ("smm", 0, 1,),
+    ("smm", 0, 2,),
+    ("smm", 0, 3,),
+    ("KI", 2,),
+    ("mult", 3,),
+    ("qv", 1,),
+    ("qk", 2,),
+    ("lv", 10,),
+    ("lk", 10,),
+    ("VI", 2,),
+    ("KI", 3,),
+    ("se", 0, 0, "S",),
+    ("se", 0, 1, "S",),
+    ("mult", 4,),
+    ("VI", 3,),
+    ("qv", 2,),
+    ("se", 0, 2, "S",),
+    ("se", 0, 3, "S",),
+    ("gb",),
+    ("qk", 3,),
+    ("qT", 0, 0,),
+    ("qT", 0, 1,),
+    ("lv", 11,),
+    ("lk", 11,),
+    ("KI", 4,),
+    ("VI", 4,),
+    ("qT", 1, 0,),
+    ("qT", 1, 1,),
+    ("mult", 5,),
+    ("smm", 1, 0,),
+    ("smm", 1, 1,),
+    ("smm", 1, 2,),
+    ("smm", 1, 3,),
+    ("VI", 5,),
+    ("qv", 3,),
+    ("qk", 4,),
+    ("lv", 12,),
+    ("lk", 12,),
+    ("KI", 5,),
+    ("qe", 0, 0, "S",),
+    ("qe", 0, 1, "S",),
+    ("sq", 0,),
+    ("mult", 6,),
+    ("qv", 4,),
+    ("qk", 5,),
+    ("VI", 6,),
+    ("se", 1, 2, "S",),
+    ("se", 1, 3, "S",),
+    ("se", 1, 0, "S",),
+    ("se", 1, 1, "S",),
+    ("lv", 13,),
+    ("lk", 13,),
+    ("KI", 6,),
+    ("mult", 7,),
+    ("qv", 5,),
+    ("qk", 6,),
+    ("qe", 1, 0, "S",),
+    ("qe", 1, 1, "S",),
+    ("KI", 7,),
+    ("mult", 8,),
+    ("qv", 6,),
+    ("smm", 2, 0,),
+    ("smm", 2, 1,),
+    ("smm", 2, 2,),
+    ("smm", 2, 3,),
+    ("qk", 7,),
+    ("sq", 1,),
+    ("VI", 7,),
+    ("qq", 0,),
+    ("KI", 8,),
+    ("mult", 9,),
+    ("qv", 7,),
+    ("qk", 8,),
+    ("KI", 9,),
+    ("qq", 1,),
+    ("VI", 8,),
+    ("mult", 10,),
+    ("qv", 8,),
+    ("qk", 9,),
+    ("se", 2, 0, "S",),
+    ("se", 2, 1, "S",),
+    ("gc",),
+    ("KI", 10,),
+    ("VI", 9,),
+    ("mult", 11,),
+    ("rmm", 0, 2,),
+    ("rmm", 0, 3,),
+    ("qv", 9,),
+    ("qk", 10,),
+    ("VI", 10,),
+    ("KI", 11,),
+    ("mult", 12,),
+    ("gate", 0, 2, 0, "S",),
+    ("gate", 0, 3, 0, "S",),
+    ("rmm", 0, 0,),
+    ("rmm", 0, 1,),
+    ("qv", 10,),
+    ("qk", 11,),
+    ("KI", 12,),
+    ("se", 2, 2, "S",),
+    ("se", 2, 3, "S",),
+    ("rmm", 1, 2,),
+    ("rmm", 1, 3,),
+    ("gate", 1, 2, 1,),
+    ("gate", 1, 3, 1,),
+    ("VI", 11,),
+    ("gate", 0, 0, 0, "S",),
+    ("gate", 0, 1, 0, "S",),
+    ("smm", 3, 0,),
+    ("smm", 3, 1,),
+    ("smm", 3, 2,),
+    ("smm", 3, 3,),
+    ("mult", 13,),
+    ("qv", 11,),
+    ("se", 3, 0, "S",),
+    ("se", 3, 1, "S",),
+    ("VI", 12,),
+    ("rmm", 1, 0,),
+    ("rmm", 1, 1,),
+    ("sq", 2,),
+    ("rmm", 2, 0,),
+    ("rmm", 2, 1,),
+    ("se", 3, 2, "S",),
+    ("se", 3, 3, "S",),
+    ("qk", 12,),
+    ("KI", 13,),
+    ("gate", 1, 0, 1,),
+    ("gate", 1, 1, 1,),
+    ("gate", 2, 0, 0, "S",),
+    ("gate", 2, 1, 0, "S",),
+    ("sq", 3,),
+    ("VI", 13,),
+    ("qv", 12,),
+    ("rmm", 3, 0,),
+    ("rmm", 3, 1,),
+    ("gate", 3, 0, 2,),
+    ("gate", 3, 1, 2,),
+    ("qk", 13,),
+    ("smm", 4, 0,),
+    ("smm", 4, 1,),
+    ("smm", 4, 2,),
+    ("smm", 4, 3,),
+    ("se", 4, 0, "V",),
+    ("se", 4, 1, "V",),
+    ("qv", 13,),
+    ("rmm", 3, 2,),
+    ("rmm", 3, 3,),
+    ("rmm", 2, 2,),
+    ("rmm", 2, 3,),
+    ("se", 4, 2, "S",),
+    ("se", 4, 3, "S",),
+    ("sq", 4,),
+    ("smm", 5, 0,),
+    ("smm", 5, 1,),
+    ("smm", 5, 2,),
+    ("smm", 5, 3,),
+    ("gate", 2, 2, 0, "S",),
+    ("gate", 2, 3, 0, "S",),
+    ("gate", 3, 2, 2,),
+    ("gate", 3, 3, 2,),
+    ("se", 5, 2, "V",),
+    ("se", 5, 3, "V",),
+    ("oT", 0, 2,),
+    ("rmm", 4, 0,),
+    ("rmm", 4, 1,),
+    ("oT", 0, 1,),
+    ("se", 5, 0, "S",),
+    ("se", 5, 1, "S",),
+    ("oe", 0, 2, "S",),
+    ("gate", 4, 0, 1,),
+    ("gate", 4, 1, 1,),
+    ("oe", 0, 1, "S",),
+    ("sq", 5,),
+    ("oT", 0, 0,),
+    ("oe", 0, 0, "S",),
+    ("rmm", 4, 2,),
+    ("rmm", 4, 3,),
+    ("gate", 4, 2, 1,),
+    ("gate", 4, 3, 1,),
+    ("oT", 0, 3,),
+    ("oe", 0, 3, "S",),
+    ("rmm", 5, 2,),
+    ("rmm", 5, 3,),
+    ("gate", 5, 2, 2,),
+    ("gate", 5, 3, 2,),
+    ("rmm", 5, 0,),
+    ("rmm", 5, 1,),
+    ("oT", 1, 2,),
+    ("gate", 5, 0, 2,),
+    ("gate", 5, 1, 2,),
+    ("oq", 0, 1,),
+    ("oq", 0, 0,),
+    ("oe", 1, 2, "S",),
+    ("oT", 1, 3,),
+    ("oe", 1, 3, "S",),
+    ("oq", 1, 1,),
+    ("oT", 1, 0,),
+    ("oT", 1, 1,),
+    ("oe", 1, 1, "S",),
+    ("oe", 1, 0, "V",),
+    ("oq", 1, 0,),
+)
+
+
+def program():
+    chunks = []
+    for b, (h, l) in enumerate(BUCKETS):
+        for i in range(LENS[l] // PASS):
+            chunks.append((h, STARTS[l] // PASS + i, b))
+    return chunks, JOBS
+
+
+def tile_loglinearfenwickbucketread_x1_kernel(tc, q, k, v, wdec, lam, out_0, out_1, out_2):
+    nc = tc.nc
+    chunks, jobs = program()
+    per_head = PAST // PASS
+
+    with ExitStack() as ctx:
+        keep = ctx.enter_context(tc.tile_pool(name="keep", bufs=1))
+        raw = ctx.enter_context(tc.tile_pool(name="raw", bufs=AHEAD))
+        mid = ctx.enter_context(tc.tile_pool(name="mid", bufs=4))
+        codes = ctx.enter_context(tc.tile_pool(name="codes", bufs=7))
+        two = ctx.enter_context(tc.tile_pool(name="two", bufs=2))
+        psum1 = ctx.enter_context(tc.psum_pool(name="psum1", bufs=1))
+        psum2 = ctx.enter_context(tc.psum_pool(name="psum2", bufs=4))
+        states = ctx.enter_context(tc.tile_pool(name="states", bufs=len(BUCKETS)))
+        ctx.enter_context(tc.manual_schedule())
+
+        ident = keep.tile([P, P], F32, name="ident")
+        make_identity(nc, ident[:])
+
+        w_raw = keep.tile([P, H * per_head, 16], BF16, name="w_raw")
+        lam_raw = keep.tile([P, H * TT, 16], BF16, name="lam_raw")
+        nc.scalar.dma_start(out=lam_raw[:, :, 0:3], in_=lam.rearrange("h (a p) l -> p (h a) l", p=P))
+        neg_abs = keep.tile([P, H * TT, 3], F32, name="neg_abs")
+        expo = keep.tile([P, H * TT, 3], F32, name="expo")
+        logt = keep.tile([P, H * TT, 3], F32, name="logt")
+        soft = keep.tile([P, H * TT, 3], F32, name="soft")
+        gate = keep.tile([P, H * TT, 3], F32, name="gate")
+        out_codes = keep.tile([P, H * C], U32, name="out_codes", align_bytes=64)
+        out_scales = keep.tile([P, H * C], U8, name="out_scales", align_bytes=64)
+
+        k_raw, v_raw, v_mul, k_grp, v_grp = {}, {}, {}, {}, {}
+        k_codes, k_scales, v_codes, v_scales = {}, {}, {}, {}
+        q_raw, q_grp, q_codes, q_scales = {}, {}, {}, {}
+        s_bank, s_grp, s_codes, s_scales = {}, {}, {}, {}
+        acc, o_grp, banks = {}, {}, {}
+
+        def lv(c):
+            h, i, b = chunks[c]
+            if c == 0 or chunks[c - 1][2] != b:
+                n = LENS[BUCKETS[b][1]]
+                nc.sync.dma_start(out=w_raw[:, h * per_head + i:h * per_head + i + n // PASS, 0:PACK],
+                                  in_=wdec[h, i * PASS:i * PASS + n].rearrange("(c p j) -> p c j", p=P, j=PACK))
+            v_raw[c] = raw.tile([P, PACK, E], BF16, name="v_raw")
+            nc.sync.dma_start(out=v_raw[c][:], in_=v[h, i * PASS:(i + 1) * PASS, :].rearrange("(p j) e -> p j e", j=PACK))
+
+        def lk(c):
+            h, i, b = chunks[c]
+            k_raw[c] = raw.tile([P, PACK, D], BF16, name="k_raw")
+            nc.sync.dma_start(out=k_raw[c][:], in_=k[h, i * PASS:(i + 1) * PASS, :].rearrange("(p j) d -> p j d", j=PACK))
+
+        def load_q(h):
+            q_raw[h] = two.tile([P, TT, D], BF16, name="q_raw")
+            nc.sync.dma_start(out=q_raw[h][:], in_=q[h].rearrange("(a p) d -> p a d", p=P))
+
+        def gates_a():
+            lam_v = lam_raw[:, :, 0:3]
+            nc.vector.scalar_tensor_tensor(out=neg_abs[:], in0=lam_v, scalar=-1.0, in1=lam_v, op0=ALU.mult, op1=ALU.min)
+            nc.scalar.activation(out=expo[:], in_=neg_abs[:], func=ACT.Exp)
+            nc.scalar.activation(out=logt[:], in_=expo[:], func=ACT.Ln, bias=1.0)
+
+        def gates_b():
+            nc.vector.scalar_tensor_tensor(out=soft[:], in0=lam_raw[:, :, 0:3], scalar=0.0, in1=logt[:], op0=ALU.max, op1=ALU.add)
+
+        def gates_c():
+            nc.vector.tensor_scalar(out=gate[:], in0=soft[:], scalar1=D ** -0.5, scalar2=None, op0=ALU.mult)
+
+        def mult(c):
+            h, i, b = chunks[c]
+            v_mul[c] = mid.tile([P, PACK, E], BF16, name="v_mul")
+            for j in range(PACK):
+                nc.vector.tensor_scalar(out=v_mul[c][:, j, :], in0=v_raw[c][:, j, :],
+                                        scalar1=w_raw[:, h * per_head + i, j:j + 1], scalar2=None, op0=ALU.mult)
+
+        def copy(eng, out, in_):
+            if eng == "S":
+                nc.scalar.copy(out=out, in_=in_)
+            else:
+                nc.vector.tensor_copy(out=out, in_=in_)
+
+        def vint(c, lo=0, hi=E, eng="S"):
+            if c not in v_grp:
+                v_grp[c] = mid.tile([P, E * PACK], BF16, name="v_grp", align_bytes=64)
+            copy(eng, v_grp[c][:, lo * PACK:hi * PACK].rearrange("p (e i j) -> p e j i", i=4, j=PACK),
+                 v_mul[c][:, :, lo:hi].rearrange("p j (e i) -> p e j i", i=4))
+
+        def kint(c, lo=0, hi=D, eng="V"):
+            if c not in k_grp:
+                k_grp[c] = mid.tile([P, D * PACK], BF16, name="k_grp", align_bytes=64)
+            dst = k_grp[c][:].rearrange("p (t a b j) -> p a t b j", t=PACK, b=2, j=PACK)
+            copy(eng, dst[:, lo // 8:hi // 8], k_raw[c][:, :, lo:hi].rearrange("p j (a b t) -> p a t b j", t=PACK, b=2))
+
+        def qk(c):
+            k_codes[c] = codes.tile([P, D], U32, name="k_codes", align_bytes=64)
+            k_scales[c] = codes.tile([P, D], U8, name="k_scales", align_bytes=64)
+            nc.vector.quantize_mx(out=k_codes[c][:].bitcast(FP8X4), scales=k_scales[c][:], in_=k_grp[c][:])
+
+        def qv(c):
+            v_codes[c] = codes.tile([P, E], U32, name="v_codes", align_bytes=64)
+            v_scales[c] = codes.tile([P, E], U8, name="v_scales", align_bytes=64)
+            nc.vector.quantize_mx(out=v_codes[c][:].bitcast(FP8X4), scales=v_scales[c][:], in_=v_grp[c][:])
+
+        def q_t(h, half):
+            banks["q", h, half] = psum2.tile([P, 2, 2, P], F32, name="bank")
+            for a in range(2):
+                words = q_raw[h][:, 2 * half + a, :].bitcast(F32)
+                for u in range(2):
+                    nc.tensor.transpose(banks["q", h, half][:, a, u, :], words[:, u:D // 2:2], ident[:])
+
+        def q_e(h, half, eng="S"):
+            if h not in q_grp:
+                q_grp[h] = two.tile([P, C * PACK], BF16, name="q_grp", align_bytes=64)
+            dst = q_grp[h][:].bitcast(F32)[:, half * PASS:(half + 1) * PASS]
+            copy(eng, dst.rearrange("p (a r u) -> p a r u", a=2, u=2), banks["q", h, half][:].rearrange("p a u r -> p a r u"))
+
+        def qq(h):
+            q_codes[h] = two.tile([P, C], U32, name="q_codes", align_bytes=64)
+            q_scales[h] = two.tile([P, C], U8, name="q_scales", align_bytes=64)
+            nc.vector.quantize_mx(out=q_codes[h][:].bitcast(FP8X4), scales=q_scales[h][:], in_=q_grp[h][:])
+
+        def smm(b, ec):
+            passes = [c for c in range(len(chunks)) if chunks[c][2] == b]
+            s_bank[b, ec] = psum1.tile([P, PACK, P], F32, name="state%d" % ec)
+            cols = slice(ec * P, (ec + 1) * P)
+            for t in range(PACK):
+                rows = slice(t * P, (t + 1) * P)
+                for c in passes:
+                    nc.tensor.matmul_mx(
+                        out=s_bank[b, ec][:, t, :],
+                        lhsT=k_codes[c][:, rows].bitcast(FP8X4), lhsT_scale=k_scales[c][:, rows],
+                        rhs=v_codes[c][:, cols].bitcast(FP8X4), rhs_scale=v_scales[c][:, cols],
+                        start=(c == passes[0]), stop=(c == passes[-1]))
+
+        def sevac(b, ec, eng="S"):
+            if b not in s_grp:
+                s_grp[b] = two.tile([P, E * PACK], BF16, name="s_grp", align_bytes=64)
+            dst = s_grp[b][:, ec * PASS:(ec + 1) * PASS].rearrange("p (e t) -> p e t", t=PACK)
+            src = s_bank[b, ec][:].rearrange("p t e -> p e t")
+            scale = LENS[BUCKETS[b][1]] ** -0.5
+            if eng == "S":
+                nc.scalar.activation(out=dst, in_=src, func=ACT.Copy, scale=scale)
+            else:
+                nc.vector.tensor_scalar(out=dst, in0=src, scalar1=scale, scalar2=None, op0=ALU.mult)
+
+        def sq(b):
+            s_codes[b] = states.tile([P, E], U32, name="s_codes", align_bytes=64)
+            s_scales[b] = states.tile([P, E], U8, name="s_scales", align_bytes=64)
+            nc.vector.quantize_mx(out=s_codes[b][:].bitcast(FP8X4), scales=s_scales[b][:], in_=s_grp[b][:])
+
+        def rmm(b, tt):
+            h, l = BUCKETS[b]
+            banks["r", b, tt] = psum2.tile([P, E], F32, name="bank")
+            rows = slice(tt * P, (tt + 1) * P)
+            nc.tensor.matmul_mx(
+                out=banks["r", b, tt][:],
+                lhsT=q_codes[h][:, rows].bitcast(FP8X4), lhsT_scale=q_scales[h][:, rows],
+                rhs=s_codes[b][:].bitcast(FP8X4), rhs_scale=s_scales[b][:],
+                start=True, stop=True)
+
+        def gated(b, tt, level, eng="V"):
+            h, l = BUCKETS[b]
+            if h not in acc:
+                acc[h] = two.tile([P, TT, E], F32, name="acc")
+            bank = banks["r", b, tt]
+            g = gate[:, h * TT + tt, l:l + 1]
+            if level == 0 and eng == "S":
+                nc.scalar.activation(out=acc[h][:, tt, :], in_=bank[:], func=ACT.Copy, scale=g)
+            elif level == 0:
+                nc.vector.tensor_scalar(out=acc[h][:, tt, :], in0=bank[:], scalar1=g, scalar2=None, op0=ALU.mult)
+            else:
+                nc.vector.scalar_tensor_tensor(out=acc[h][:, tt, :], in0=bank[:], scalar=g, in1=acc[h][:, tt, :],
+                                               op0=ALU.mult, op1=ALU.add)
+            if level == 2:
+                nc.sync.dma_start(out=out_0[h, tt * P:(tt + 1) * P, :], in_=acc[h][:, tt, :])
+
+        def o_t(h, tt):
+            banks["o", h, tt] = psum2.tile([P, PACK, P], F32, name="bank")
+            for j in range(PACK):
+                nc.tensor.transpose(banks["o", h, tt][:, j, :], acc[h][:, tt, j:E:PACK], ident[:])
+
+        def o_e(h, tt, eng="S"):
+            if h not in o_grp:
+                o_grp[h] = two.tile([P, C * PACK], BF16, name="o_grp", align_bytes=64)
+            dst = o_grp[h][:, tt * PASS:(tt + 1) * PASS]
+            copy(eng, dst.rearrange("p (r j) -> p r j", j=PACK), banks["o", h, tt][:].rearrange("p j r -> p r j"))
+
+        def oq(h, half):
+            cols = slice(h * C + half * C // 2, h * C + (half + 1) * C // 2)
+            nc.vector.quantize_mx(out=out_codes[:, cols].bitcast(FP8X4), scales=out_scales[:, cols], in_=o_grp[h][:, half * 2 * C:(half + 1) * 2 * C])
+            words = out_1[0].rearrange("p m t -> p (m t)").bitcast(I32)
+            nc.sync.dma_start(out=words[:, cols], in_=out_codes[:, cols].bitcast(I32))
+
+        def store_scales():
+            for quad in range(4):
+                queue = nc.scalar if quad % 2 else nc.sync
+                queue.dma_start(out=out_2[0, 4 * quad:4 * quad + 4, :].bitcast(I32),
+                                in_=out_scales[32 * quad:32 * quad + 4, :].bitcast(I32))
+
+        table = {"lv": lv, "lk": lk, "lq": load_q, "ga": gates_a, "gb": gates_b, "gc": gates_c, "mult": mult,
+                 "VI": vint, "KI": kint, "qk": qk, "qv": qv, "qT": q_t, "qe": q_e, "qq": qq, "smm": smm,
+                 "se": sevac, "sq": sq, "rmm": rmm, "gate": gated, "oT": o_t, "oe": o_e, "oq": oq}
+        for job in jobs:
+            table[job[0]](*job[1:])
+        store_scales()

@@ -22,245 +22,8 @@ PAST = sum(LENS)
 TT = C // P
 FLOPS = 2 * H * (PAST * D * E + 3 * C * D * E)
 
-AHEAD = 8
+AHEAD = 7
 BUCKETS = ((0, 2), (0, 1), (1, 0), (0, 0), (1, 1), (1, 2))
-JOBS = (
-    ("lv", 0,),
-    ("lk", 0,),
-    ("lv", 1,),
-    ("lk", 1,),
-    ("lv", 2,),
-    ("lk", 2,),
-    ("lv", 3,),
-    ("lk", 3,),
-    ("lq", 0,),
-    ("lv", 4,),
-    ("lk", 4,),
-    ("lv", 5,),
-    ("lk", 5,),
-    ("lv", 6,),
-    ("lk", 6,),
-    ("lv", 7,),
-    ("lk", 7,),
-    ("ga",),
-    ("lq", 1,),
-    ("mult", 0,),
-    ("KI", 0,),
-    ("mult", 1,),
-    ("qk", 0,),
-    ("VI", 0,),
-    ("lv", 8,),
-    ("lk", 8,),
-    ("VI", 1,),
-    ("KI", 1,),
-    ("mult", 2,),
-    ("qv", 0,),
-    ("qk", 1,),
-    ("lv", 9,),
-    ("lk", 9,),
-    ("smm", 0, 0,),
-    ("smm", 0, 1,),
-    ("smm", 0, 2,),
-    ("smm", 0, 3,),
-    ("KI", 2,),
-    ("mult", 3,),
-    ("qv", 1,),
-    ("qk", 2,),
-    ("lv", 10,),
-    ("lk", 10,),
-    ("VI", 2,),
-    ("KI", 3,),
-    ("se", 0, 0, "S",),
-    ("se", 0, 1, "S",),
-    ("mult", 4,),
-    ("VI", 3,),
-    ("qv", 2,),
-    ("se", 0, 2, "S",),
-    ("se", 0, 3, "S",),
-    ("gb",),
-    ("qk", 3,),
-    ("qT", 0, 0,),
-    ("qT", 0, 1,),
-    ("lv", 11,),
-    ("lk", 11,),
-    ("KI", 4,),
-    ("VI", 4,),
-    ("qT", 1, 0,),
-    ("qT", 1, 1,),
-    ("mult", 5,),
-    ("smm", 1, 0,),
-    ("smm", 1, 1,),
-    ("smm", 1, 2,),
-    ("smm", 1, 3,),
-    ("VI", 5,),
-    ("qv", 3,),
-    ("qk", 4,),
-    ("lv", 12,),
-    ("lk", 12,),
-    ("KI", 5,),
-    ("qe", 0, 0, "S",),
-    ("qe", 0, 1, "S",),
-    ("sq", 0,),
-    ("mult", 6,),
-    ("qv", 4,),
-    ("qk", 5,),
-    ("VI", 6,),
-    ("se", 1, 2, "S",),
-    ("se", 1, 3, "S",),
-    ("se", 1, 0, "S",),
-    ("se", 1, 1, "S",),
-    ("lv", 13,),
-    ("lk", 13,),
-    ("KI", 6,),
-    ("mult", 7,),
-    ("qv", 5,),
-    ("qk", 6,),
-    ("qe", 1, 0, "S",),
-    ("qe", 1, 1, "S",),
-    ("KI", 7,),
-    ("mult", 8,),
-    ("qv", 6,),
-    ("smm", 2, 0,),
-    ("smm", 2, 1,),
-    ("smm", 2, 2,),
-    ("smm", 2, 3,),
-    ("qk", 7,),
-    ("sq", 1,),
-    ("VI", 7,),
-    ("qq", 0,),
-    ("KI", 8,),
-    ("mult", 9,),
-    ("qv", 7,),
-    ("qk", 8,),
-    ("KI", 9,),
-    ("qq", 1,),
-    ("VI", 8,),
-    ("mult", 10,),
-    ("qv", 8,),
-    ("qk", 9,),
-    ("se", 2, 0, "S",),
-    ("se", 2, 1, "S",),
-    ("gc",),
-    ("KI", 10,),
-    ("VI", 9,),
-    ("mult", 11,),
-    ("rmm", 0, 2,),
-    ("rmm", 0, 3,),
-    ("qv", 9,),
-    ("qk", 10,),
-    ("VI", 10,),
-    ("KI", 11,),
-    ("mult", 12,),
-    ("gate", 0, 2, 0, "S",),
-    ("gate", 0, 3, 0, "S",),
-    ("rmm", 0, 0,),
-    ("rmm", 0, 1,),
-    ("qv", 10,),
-    ("qk", 11,),
-    ("KI", 12,),
-    ("se", 2, 2, "S",),
-    ("se", 2, 3, "S",),
-    ("rmm", 1, 2,),
-    ("rmm", 1, 3,),
-    ("gate", 1, 2, 1,),
-    ("gate", 1, 3, 1,),
-    ("VI", 11,),
-    ("gate", 0, 0, 0, "S",),
-    ("gate", 0, 1, 0, "S",),
-    ("smm", 3, 0,),
-    ("smm", 3, 1,),
-    ("smm", 3, 2,),
-    ("smm", 3, 3,),
-    ("mult", 13,),
-    ("qv", 11,),
-    ("se", 3, 0, "S",),
-    ("se", 3, 1, "S",),
-    ("VI", 12,),
-    ("rmm", 1, 0,),
-    ("rmm", 1, 1,),
-    ("sq", 2,),
-    ("rmm", 2, 0,),
-    ("rmm", 2, 1,),
-    ("se", 3, 2, "S",),
-    ("se", 3, 3, "S",),
-    ("qk", 12,),
-    ("KI", 13,),
-    ("gate", 1, 0, 1,),
-    ("gate", 1, 1, 1,),
-    ("gate", 2, 0, 0, "S",),
-    ("gate", 2, 1, 0, "S",),
-    ("sq", 3,),
-    ("VI", 13,),
-    ("qv", 12,),
-    ("rmm", 3, 0,),
-    ("rmm", 3, 1,),
-    ("gate", 3, 0, 2,),
-    ("gate", 3, 1, 2,),
-    ("qk", 13,),
-    ("smm", 4, 0,),
-    ("smm", 4, 1,),
-    ("smm", 4, 2,),
-    ("smm", 4, 3,),
-    ("se", 4, 0, "V",),
-    ("se", 4, 1, "V",),
-    ("qv", 13,),
-    ("rmm", 3, 2,),
-    ("rmm", 3, 3,),
-    ("rmm", 2, 2,),
-    ("rmm", 2, 3,),
-    ("se", 4, 2, "S",),
-    ("se", 4, 3, "S",),
-    ("sq", 4,),
-    ("smm", 5, 0,),
-    ("smm", 5, 1,),
-    ("smm", 5, 2,),
-    ("smm", 5, 3,),
-    ("gate", 2, 2, 0, "S",),
-    ("gate", 2, 3, 0, "S",),
-    ("gate", 3, 2, 2,),
-    ("gate", 3, 3, 2,),
-    ("se", 5, 2, "V",),
-    ("se", 5, 3, "V",),
-    ("oT", 0, 2,),
-    ("rmm", 4, 0,),
-    ("rmm", 4, 1,),
-    ("oT", 0, 1,),
-    ("se", 5, 0, "S",),
-    ("se", 5, 1, "S",),
-    ("oe", 0, 2, "S",),
-    ("gate", 4, 0, 1,),
-    ("gate", 4, 1, 1,),
-    ("oe", 0, 1, "S",),
-    ("sq", 5,),
-    ("oT", 0, 0,),
-    ("oe", 0, 0, "S",),
-    ("rmm", 4, 2,),
-    ("rmm", 4, 3,),
-    ("gate", 4, 2, 1,),
-    ("gate", 4, 3, 1,),
-    ("oT", 0, 3,),
-    ("oe", 0, 3, "S",),
-    ("rmm", 5, 2,),
-    ("rmm", 5, 3,),
-    ("gate", 5, 2, 2,),
-    ("gate", 5, 3, 2,),
-    ("rmm", 5, 0,),
-    ("rmm", 5, 1,),
-    ("oT", 1, 2,),
-    ("gate", 5, 0, 2,),
-    ("gate", 5, 1, 2,),
-    ("oq", 0, 1,),
-    ("oq", 0, 0,),
-    ("oe", 1, 2, "S",),
-    ("oT", 1, 3,),
-    ("oe", 1, 3, "S",),
-    ("oq", 1, 1,),
-    ("oT", 1, 0,),
-    ("oT", 1, 1,),
-    ("oe", 1, 1, "S",),
-    ("oe", 1, 0, "V",),
-    ("oq", 1, 0,),
-)
 
 
 def program():
@@ -268,7 +31,62 @@ def program():
     for b, (h, l) in enumerate(BUCKETS):
         for i in range(LENS[l] // PASS):
             chunks.append((h, STARTS[l] // PASS + i, b))
-    return chunks, JOBS
+    n = len(chunks)
+
+    def smm(b):
+        return [("smm", b, ec) for ec in range(4)]
+
+    def se(b, parts=range(4), eng="S"):
+        return [("se", b, ec, eng) for ec in parts]
+
+    def rmm(b, tiles=range(4)):
+        return [("rmm", b, tt) for tt in tiles]
+
+    def gate(b, level, tiles=range(4)):
+        return [("gate", b, tt, level) + (("S",) if level == 0 else ()) for tt in tiles]
+
+    def qT(h):
+        return [("qT", h, 0), ("qT", h, 1)]
+
+    def qe(h):
+        return [("qe", h, 0, "S"), ("qe", h, 1, "S")]
+
+    extra = {
+        1: smm(0) + qT(0),
+        2: se(0) + [("gb",)],
+        3: qe(0) + smm(1) + [("gc",)],
+        4: se(1, (0, 1)) + [("sq", 0)],
+        5: se(1, (2, 3)) + [("qq", 0)] + qT(1),
+        6: qe(1) + rmm(0),
+        7: smm(2) + gate(0, 0, (0, 1)) + [("sq", 1)],
+        8: gate(0, 0, (2, 3)) + [("qq", 1)] + rmm(1, (0, 1)),
+        9: se(2) + gate(1, 1, (0, 1)),
+        10: [("sq", 2)] + rmm(2, (0, 1)) + rmm(1, (2, 3)),
+        11: smm(3) + gate(2, 0, (0, 1)),
+        12: se(3, (0, 1, 2)) + rmm(2, (2, 3)),
+    }
+    jobs = []
+    for c in range(AHEAD):
+        jobs += [("lv", c), ("lk", c)]
+        if c in (2, 5):
+            jobs.append(("lq", c // 4))
+    jobs += [("ga",), ("mult", 0)]
+    for s in range(n - 1):
+        if s >= 1 and s + AHEAD - 1 < n:
+            jobs += [("lv", s + AHEAD - 1), ("lk", s + AHEAD - 1)]
+        jobs += [("VP", s, 0, 4, "S"), ("KP", s, 0, 4, "V"), ("mult", s + 1)]
+        jobs.append(("Q", s) if s else ("qk", s))
+        jobs += extra.get(s, [])
+    s = n - 1
+    jobs += [("VP", s, 0, 2, "S"), ("KP", s, 0, 4, "V"), ("VP", s, 2, 4, "V"), ("Q", s)] + se(3, (3,), "V") + gate(1, 1, (2, 3)) + [("sq", 3)] + smm(4)
+    jobs += [("qv", s)] + se(4) + rmm(3, (0, 1)) + gate(2, 0, (2, 3)) + smm(5) + rmm(3, (2, 3))
+    jobs += gate(3, 2, (0, 1)) + [("sq", 4)] + gate(3, 2, (2, 3)) + se(5) + rmm(4)
+    jobs += gate(4, 1, (0, 1)) + [("sq", 5)] + gate(4, 1, (2, 3))
+    jobs += [("oc", 0, tt, "S") for tt in range(4)] + [("oT", 0, 0), ("oT", 0, 1)] + rmm(5, (0, 1)) + [("oe", 0, 0, "S")]
+    jobs += rmm(5, (2, 3)) + gate(5, 2) + [("oT", 0, 2), ("oT", 0, 3)]
+    jobs += [("oc", 1, tt, "S") for tt in range(3)] + [("oc", 1, 3, "V"), ("oe", 0, 1, "S"), ("oq", 0, 0), ("oq", 0, 1)]
+    jobs += [("oT", 1, tt) for tt in range(4)] + [("oe", 1, 0, "S"), ("oe", 1, 1, "S"), ("oq", 1, 0), ("oq", 1, 1)]
+    return chunks, jobs
 
 
 def tile_loglinearfenwickbucketread_x1_kernel(tc, q, k, v, wdec, lam, out_0, out_1, out_2):
@@ -280,7 +98,7 @@ def tile_loglinearfenwickbucketread_x1_kernel(tc, q, k, v, wdec, lam, out_0, out
         keep = ctx.enter_context(tc.tile_pool(name="keep", bufs=1))
         raw = ctx.enter_context(tc.tile_pool(name="raw", bufs=AHEAD))
         mid = ctx.enter_context(tc.tile_pool(name="mid", bufs=4))
-        codes = ctx.enter_context(tc.tile_pool(name="codes", bufs=7))
+        codes = ctx.enter_context(tc.tile_pool(name="codes", bufs=8))
         two = ctx.enter_context(tc.tile_pool(name="two", bufs=2))
         psum1 = ctx.enter_context(tc.psum_pool(name="psum1", bufs=1))
         psum2 = ctx.enter_context(tc.psum_pool(name="psum2", bufs=4))
@@ -291,21 +109,21 @@ def tile_loglinearfenwickbucketread_x1_kernel(tc, q, k, v, wdec, lam, out_0, out
         make_identity(nc, ident[:])
 
         w_raw = keep.tile([P, H * per_head, 16], BF16, name="w_raw")
-        lam_raw = keep.tile([P, H * TT, 16], BF16, name="lam_raw")
-        nc.scalar.dma_start(out=lam_raw[:, :, 0:3], in_=lam.rearrange("h (a p) l -> p (h a) l", p=P))
-        neg_abs = keep.tile([P, H * TT, 3], F32, name="neg_abs")
-        expo = keep.tile([P, H * TT, 3], F32, name="expo")
-        logt = keep.tile([P, H * TT, 3], F32, name="logt")
-        soft = keep.tile([P, H * TT, 3], F32, name="soft")
-        gate = keep.tile([P, H * TT, 3], F32, name="gate")
+        lam_raw = keep.tile([P, H * 2, 16], BF16, name="lam_raw")
+        nc.scalar.dma_start(out=lam_raw[:, :, 0:6], in_=lam.rearrange("h (f p a) l -> p (h f) (a l)", p=P, a=2))
+        neg_abs = keep.tile([P, H * 2, 6], F32, name="neg_abs")
+        expo = keep.tile([P, H * 2, 6], F32, name="expo")
+        logt = keep.tile([P, H * 2, 6], F32, name="logt")
+        soft = keep.tile([P, H * 2, 6], F32, name="soft")
+        gate = keep.tile([P, H * 2, 6], F32, name="gate")
         out_codes = keep.tile([P, H * C], U32, name="out_codes", align_bytes=64)
         out_scales = keep.tile([P, H * C], U8, name="out_scales", align_bytes=64)
 
-        k_raw, v_raw, v_mul, k_grp, v_grp = {}, {}, {}, {}, {}
-        k_codes, k_scales, v_codes, v_scales = {}, {}, {}, {}
+        k_raw, v_raw, v_mul, kv_grp = {}, {}, {}, {}
+        kv_codes, kv_scales = {}, {}
         q_raw, q_grp, q_codes, q_scales = {}, {}, {}, {}
         s_bank, s_grp, s_codes, s_scales = {}, {}, {}, {}
-        acc, o_grp, banks = {}, {}, {}
+        acc, o_grp, banks, o_bf = {}, {}, {}, {}
 
         def lv(c):
             h, i, b = chunks[c]
@@ -323,16 +141,16 @@ def tile_loglinearfenwickbucketread_x1_kernel(tc, q, k, v, wdec, lam, out_0, out
 
         def load_q(h):
             q_raw[h] = two.tile([P, TT, D], BF16, name="q_raw")
-            nc.sync.dma_start(out=q_raw[h][:], in_=q[h].rearrange("(a p) d -> p a d", p=P))
+            nc.sync.dma_start(out=q_raw[h][:].rearrange("p (f a) d -> p f a d", a=2), in_=q[h].rearrange("(f p a) d -> p f a d", p=P, a=2))
 
         def gates_a():
-            lam_v = lam_raw[:, :, 0:3]
+            lam_v = lam_raw[:, :, 0:6]
             nc.vector.scalar_tensor_tensor(out=neg_abs[:], in0=lam_v, scalar=-1.0, in1=lam_v, op0=ALU.mult, op1=ALU.min)
             nc.scalar.activation(out=expo[:], in_=neg_abs[:], func=ACT.Exp)
             nc.scalar.activation(out=logt[:], in_=expo[:], func=ACT.Ln, bias=1.0)
 
         def gates_b():
-            nc.vector.scalar_tensor_tensor(out=soft[:], in0=lam_raw[:, :, 0:3], scalar=0.0, in1=logt[:], op0=ALU.max, op1=ALU.add)
+            nc.vector.scalar_tensor_tensor(out=soft[:], in0=lam_raw[:, :, 0:6], scalar=0.0, in1=logt[:], op0=ALU.max, op1=ALU.add)
 
         def gates_c():
             nc.vector.tensor_scalar(out=gate[:], in0=soft[:], scalar1=D ** -0.5, scalar2=None, op0=ALU.mult)
@@ -347,30 +165,37 @@ def tile_loglinearfenwickbucketread_x1_kernel(tc, q, k, v, wdec, lam, out_0, out
         def copy(eng, out, in_):
             if eng == "S":
                 nc.scalar.copy(out=out, in_=in_)
+            elif eng == "G":
+                nc.gpsimd.tensor_scalar(out=out, in0=in_, scalar1=1.0, scalar2=1.0, op0=ALU.mult, op1=ALU.mult)
             else:
                 nc.vector.tensor_copy(out=out, in_=in_)
 
-        def vint(c, lo=0, hi=E, eng="S"):
-            if c not in v_grp:
-                v_grp[c] = mid.tile([P, E * PACK], BF16, name="v_grp", align_bytes=64)
-            copy(eng, v_grp[c][:, lo * PACK:hi * PACK].rearrange("p (e i j) -> p e j i", i=4, j=PACK),
+        def grouped(s):
+            if s not in kv_grp:
+                kv_grp[s] = mid.tile([P, (D + E) * PACK], BF16, name="kv_grp", align_bytes=64)
+            return kv_grp[s]
+
+        def vint(c, lo, hi, eng):
+            lo, hi = lo * P, hi * P
+            copy(eng, grouped(c + 1)[:, (D + lo) * PACK:(D + hi) * PACK].rearrange("p (e i j) -> p e j i", i=4, j=PACK),
                  v_mul[c][:, :, lo:hi].rearrange("p j (e i) -> p e j i", i=4))
 
-        def kint(c, lo=0, hi=D, eng="V"):
-            if c not in k_grp:
-                k_grp[c] = mid.tile([P, D * PACK], BF16, name="k_grp", align_bytes=64)
-            dst = k_grp[c][:].rearrange("p (t a b j) -> p a t b j", t=PACK, b=2, j=PACK)
+        def kint(c, lo, hi, eng):
+            lo, hi = lo * P, hi * P
+            dst = grouped(c)[:, 0:D * PACK].rearrange("p (t a b j) -> p a t b j", t=PACK, b=2, j=PACK)
             copy(eng, dst[:, lo // 8:hi // 8], k_raw[c][:, :, lo:hi].rearrange("p j (a b t) -> p a t b j", t=PACK, b=2))
 
+        def quant(s, lo=0, hi=D + E):
+            kv_codes[s] = codes.tile([P, D + E], U32, name="kv_codes", align_bytes=64)
+            kv_scales[s] = codes.tile([P, D + E], U8, name="kv_scales", align_bytes=64)
+            nc.vector.quantize_mx(out=kv_codes[s][:, lo:hi].bitcast(FP8X4), scales=kv_scales[s][:, lo:hi],
+                                  in_=kv_grp[s][:, lo * PACK:hi * PACK])
+
         def qk(c):
-            k_codes[c] = codes.tile([P, D], U32, name="k_codes", align_bytes=64)
-            k_scales[c] = codes.tile([P, D], U8, name="k_scales", align_bytes=64)
-            nc.vector.quantize_mx(out=k_codes[c][:].bitcast(FP8X4), scales=k_scales[c][:], in_=k_grp[c][:])
+            quant(c, 0, D)
 
         def qv(c):
-            v_codes[c] = codes.tile([P, E], U32, name="v_codes", align_bytes=64)
-            v_scales[c] = codes.tile([P, E], U8, name="v_scales", align_bytes=64)
-            nc.vector.quantize_mx(out=v_codes[c][:].bitcast(FP8X4), scales=v_scales[c][:], in_=v_grp[c][:])
+            quant(c + 1, D, D + E)
 
         def q_t(h, half):
             banks["q", h, half] = psum2.tile([P, 2, 2, P], F32, name="bank")
@@ -393,14 +218,14 @@ def tile_loglinearfenwickbucketread_x1_kernel(tc, q, k, v, wdec, lam, out_0, out
         def smm(b, ec):
             passes = [c for c in range(len(chunks)) if chunks[c][2] == b]
             s_bank[b, ec] = psum1.tile([P, PACK, P], F32, name="state%d" % ec)
-            cols = slice(ec * P, (ec + 1) * P)
+            cols = slice(D + ec * P, D + (ec + 1) * P)
             for t in range(PACK):
                 rows = slice(t * P, (t + 1) * P)
                 for c in passes:
                     nc.tensor.matmul_mx(
                         out=s_bank[b, ec][:, t, :],
-                        lhsT=k_codes[c][:, rows].bitcast(FP8X4), lhsT_scale=k_scales[c][:, rows],
-                        rhs=v_codes[c][:, cols].bitcast(FP8X4), rhs_scale=v_scales[c][:, cols],
+                        lhsT=kv_codes[c][:, rows].bitcast(FP8X4), lhsT_scale=kv_scales[c][:, rows],
+                        rhs=kv_codes[c + 1][:, cols].bitcast(FP8X4), rhs_scale=kv_scales[c + 1][:, cols],
                         start=(c == passes[0]), stop=(c == passes[-1]))
 
         def sevac(b, ec, eng="S"):
@@ -434,7 +259,7 @@ def tile_loglinearfenwickbucketread_x1_kernel(tc, q, k, v, wdec, lam, out_0, out
             if h not in acc:
                 acc[h] = two.tile([P, TT, E], F32, name="acc")
             bank = banks["r", b, tt]
-            g = gate[:, h * TT + tt, l:l + 1]
+            g = gate[:, h * 2 + tt // 2, (tt % 2) * 3 + l:(tt % 2) * 3 + l + 1]
             if level == 0 and eng == "S":
                 nc.scalar.activation(out=acc[h][:, tt, :], in_=bank[:], func=ACT.Copy, scale=g)
             elif level == 0:
@@ -443,18 +268,25 @@ def tile_loglinearfenwickbucketread_x1_kernel(tc, q, k, v, wdec, lam, out_0, out
                 nc.vector.scalar_tensor_tensor(out=acc[h][:, tt, :], in0=bank[:], scalar=g, in1=acc[h][:, tt, :],
                                                op0=ALU.mult, op1=ALU.add)
             if level == 2:
-                nc.sync.dma_start(out=out_0[h, tt * P:(tt + 1) * P, :], in_=acc[h][:, tt, :])
+                nc.sync.dma_start(out=out_0[h].rearrange("(f p a) e -> f a p e", p=P, a=2)[tt // 2, tt % 2], in_=acc[h][:, tt, :])
+
+        def o_c(h, tt, eng):
+            o_bf[h, tt] = mid.tile([P, E], BF16, name="o_bf")
+            copy(eng, o_bf[h, tt][:].rearrange("p (u r e) -> p u r e", u=2, e=2),
+                 acc[h][:, tt, :].rearrange("p (r u e) -> p u r e", u=2, e=2))
 
         def o_t(h, tt):
-            banks["o", h, tt] = psum2.tile([P, PACK, P], F32, name="bank")
-            for j in range(PACK):
-                nc.tensor.transpose(banks["o", h, tt][:, j, :], acc[h][:, tt, j:E:PACK], ident[:])
+            if ("o", h, tt // 2) not in banks:
+                banks["o", h, tt // 2] = psum2.tile([P, 2, 2, P], F32, name="bank")
+            words = o_bf[h, tt][:].bitcast(F32)
+            for u in range(2):
+                nc.tensor.transpose(banks["o", h, tt // 2][:, tt % 2, u, :], words[:, u * P:(u + 1) * P], ident[:])
 
-        def o_e(h, tt, eng="S"):
+        def o_e(h, half, eng="S"):
             if h not in o_grp:
                 o_grp[h] = two.tile([P, C * PACK], BF16, name="o_grp", align_bytes=64)
-            dst = o_grp[h][:, tt * PASS:(tt + 1) * PASS]
-            copy(eng, dst.rearrange("p (r j) -> p r j", j=PACK), banks["o", h, tt][:].rearrange("p j r -> p r j"))
+            dst = o_grp[h][:].bitcast(F32)[:, half * PASS:(half + 1) * PASS]
+            copy(eng, dst.rearrange("p (r a u) -> p r a u", a=2, u=2), banks["o", h, half][:].rearrange("p a u r -> p r a u"))
 
         def oq(h, half):
             cols = slice(h * C + half * C // 2, h * C + (half + 1) * C // 2)
@@ -469,7 +301,7 @@ def tile_loglinearfenwickbucketread_x1_kernel(tc, q, k, v, wdec, lam, out_0, out
                                 in_=out_scales[32 * quad:32 * quad + 4, :].bitcast(I32))
 
         table = {"lv": lv, "lk": lk, "lq": load_q, "ga": gates_a, "gb": gates_b, "gc": gates_c, "mult": mult,
-                 "VI": vint, "KI": kint, "qk": qk, "qv": qv, "qT": q_t, "qe": q_e, "qq": qq, "smm": smm,
+                 "VP": vint, "KP": kint, "oc": o_c, "qk": qk, "Q": quant, "qv": qv, "qT": q_t, "qe": q_e, "qq": qq, "smm": smm,
                  "se": sevac, "sq": sq, "rmm": rmm, "gate": gated, "oT": o_t, "oe": o_e, "oq": oq}
         for job in jobs:
             table[job[0]](*job[1:])

@@ -33,8 +33,8 @@ def program():
             chunks.append((h, STARTS[l] // PASS + i, b))
     n = len(chunks)
 
-    def smm(b):
-        return [("smm", b, ec) for ec in range(4)]
+    def smm(b, parts=range(4)):
+        return [("smm", b, ec) for ec in parts]
 
     def se(b, parts=range(4), eng="S"):
         return [("se", b, ec, eng) for ec in parts]
@@ -51,41 +51,45 @@ def program():
     def qe(h):
         return [("qe", h, 0, "S"), ("qe", h, 1, "S")]
 
+    back = (3, 2, 1, 0)
+    pairs = (1, 0, 3, 2)
     extra = {
-        1: smm(0) + qT(0),
-        2: se(0) + [("gb",)],
-        3: qe(0) + smm(1) + [("gc",)],
-        4: se(1, (0, 1)) + [("sq", 0)],
-        5: se(1, (2, 3)) + [("qq", 0)] + qT(1),
-        6: qe(1) + rmm(0),
-        7: smm(2) + gate(0, 0, (0, 1)) + [("sq", 1)],
-        8: gate(0, 0, (2, 3)) + [("qq", 1)] + rmm(1, (0, 1)),
-        9: se(2) + gate(1, 1, (0, 1)),
-        10: [("sq", 2)] + rmm(2, (0, 1)) + rmm(1, (2, 3)),
-        11: smm(3) + gate(2, 0, (0, 1)),
-        12: se(3, (0, 1, 2)) + rmm(2, (2, 3)),
+        1: smm(0) + [("gb",)],
+        2: se(0, pairs) + qT(0),
+        3: [("KP", 4, 2, 4, "S")] + smm(1) + [("gc",)],
+        4: qe(0)[::-1] + [("sq", 0)] + qT(1),
+        5: se(1, back),
+        6: qe(1)[::-1] + [("qq", 0)] + rmm(0),
+        7: smm(2),
+        8: [("sq", 1)] + gate(0, 0, back),
+        9: [("qq", 1)] + se(2, back) + rmm(1, (1, 0)),
+        10: [("sq", 2)] + rmm(2, (1, 0)) + [("pre", 3)],
+        11: [("smr", 3, ec) for ec in range(4)],
     }
+    shared = {4: 2}
     jobs = []
-    for c in range(AHEAD):
-        jobs += [("lv", c), ("lk", c)]
-        if c in (2, 5):
-            jobs.append(("lq", c // 4))
+    jobs += [("lv", 0), ("lk", 0), ("lv", 1), ("lk", 1), ("lv", 2), ("lk", 2), ("lv2", 3), ("lk2", 3), ("lq", 0), ("lv2", 5), ("lk2", 5), ("lq", 1)]
     jobs += [("ga",), ("mult", 0)]
     for s in range(n - 1):
-        if s >= 1 and s + AHEAD - 1 < n:
-            jobs += [("lv", s + AHEAD - 1), ("lk", s + AHEAD - 1)]
-        jobs += [("VP", s, 0, 4, "S"), ("KP", s, 0, 4, "V"), ("mult", s + 1)]
+        if s in (2, 3, 5):
+            c = {2: 7, 3: 9, 5: 11}[s]
+            jobs += [("lv2", c), ("lk2", c)]
+        if s == 7:
+            jobs += [("lv", 13), ("lk", 13)]
+        jobs += [("VP", s, 0, 4, "S"), ("KP", s, 0, shared.get(s, 4), "V"), ("mult", s + 1)]
         jobs.append(("Q", s) if s else ("qk", s))
         jobs += extra.get(s, [])
     s = n - 1
-    jobs += [("VP", s, 0, 2, "S"), ("KP", s, 0, 4, "V"), ("VP", s, 2, 4, "V"), ("Q", s)] + se(3, (3,), "V") + gate(1, 1, (2, 3)) + [("sq", 3)] + smm(4)
-    jobs += [("qv", s)] + se(4) + rmm(3, (0, 1)) + gate(2, 0, (2, 3)) + smm(5) + rmm(3, (2, 3))
-    jobs += gate(3, 2, (0, 1)) + [("sq", 4)] + gate(3, 2, (2, 3)) + se(5) + rmm(4)
-    jobs += gate(4, 1, (0, 1)) + [("sq", 5)] + gate(4, 1, (2, 3))
-    jobs += [("oc", 0, tt, "S") for tt in range(4)] + [("oT", 0, 0), ("oT", 0, 1)] + rmm(5, (0, 1)) + [("oe", 0, 0, "S")]
-    jobs += rmm(5, (2, 3)) + gate(5, 2) + [("oT", 0, 2), ("oT", 0, 3)]
-    jobs += [("oc", 1, tt, "S") for tt in range(3)] + [("oc", 1, 3, "V"), ("oe", 0, 1, "S"), ("oq", 0, 0), ("oq", 0, 1)]
-    jobs += [("oT", 1, tt) for tt in range(4)] + [("oe", 1, 0, "S"), ("oe", 1, 1, "S"), ("oq", 1, 0), ("oq", 1, 1)]
+    jobs += [("VP", s, 0, 2, "S"), ("KP", s, 0, 4, "V")] + gate(1, 1, (0, 1)) + rmm(1, (3, 2)) + [("Q", s)] + gate(2, 0, (0, 1))
+    jobs += se(3) + gate(1, 1, (2, 3)) + rmm(2, (3, 2)) + smm(4) + [("VP", s, 2, 4, "V"), ("sq", 3), ("qv", s)]
+    jobs += gate(2, 0, (2, 3)) + rmm(3, (0, 1, 3, 2)) + se(4, pairs) + smm(5, back)
+    jobs += gate(3, 2, (0, 1)) + [("sq", 4)] + gate(3, 2, (2, 3)) + [("oc", 0, 0, "S")] + se(5, (2, 3, 0, 1))
+    jobs += rmm(4, (0, 1)) + [("oT", 0, 0)] + gate(4, 1, (1, 0)) + rmm(4, (3, 2)) + [("sq", 5)] + gate(4, 1, (2, 3))
+    jobs += [("oc", 0, 1, "S"), ("oT", 0, 1), ("oc", 0, 3, "S"), ("oe", 0, 0, "S"), ("oc", 0, 2, "S")]
+    jobs += rmm(5, (0, 1)) + gate(5, 2, (0,)) + rmm(5, (3,)) + gate(5, 2, (1,)) + rmm(5, (2,)) + gate(5, 2, (2, 3)) + [("oT", 0, 2), ("oT", 0, 3)]
+    jobs += [("oc", 1, tt, "S") for tt in range(3)] + [("oc", 1, 3, "V")]
+    jobs += [("oT", 1, tt) for tt in range(4)] + [("oe", 1, 0, "S"), ("oe", 0, 1, "S"), ("oe", 1, 1, "S")]
+    jobs += [("oq", 0, 0), ("oq", 1, 0), ("oq", 0, 1), ("oq", 1, 1)]
     return chunks, jobs
 
 
@@ -96,7 +100,7 @@ def tile_loglinearfenwickbucketread_x1_kernel(tc, q, k, v, wdec, lam, out_0, out
 
     with ExitStack() as ctx:
         keep = ctx.enter_context(tc.tile_pool(name="keep", bufs=1))
-        raw = ctx.enter_context(tc.tile_pool(name="raw", bufs=AHEAD))
+        raw = ctx.enter_context(tc.tile_pool(name="raw", bufs=4))
         mid = ctx.enter_context(tc.tile_pool(name="mid", bufs=4))
         codes = ctx.enter_context(tc.tile_pool(name="codes", bufs=8))
         two = ctx.enter_context(tc.tile_pool(name="two", bufs=2))
@@ -125,19 +129,28 @@ def tile_loglinearfenwickbucketread_x1_kernel(tc, q, k, v, wdec, lam, out_0, out
         s_bank, s_grp, s_codes, s_scales = {}, {}, {}, {}
         acc, o_grp, banks, o_bf = {}, {}, {}, {}
 
-        def lv(c):
+        def fetch(src, held, name, c, count):
+            h, i, b = chunks[c]
+            if c == 1:
+                slot = held["first"][:, 1:2]
+            else:
+                pair = raw.tile([P, 2, PACK, D], BF16, name=name)
+                held["first"] = pair
+                slot = pair[:, 0:count]
+            nc.sync.dma_start(out=slot, in_=src[h, i * PASS:(i + count) * PASS, :].rearrange("(g p j) d -> p g j d", p=P, j=PACK))
+            for g in range(count):
+                held[c + g] = slot[:, g]
+
+        def lv(c, count=1):
             h, i, b = chunks[c]
             if c == 0 or chunks[c - 1][2] != b:
                 n = LENS[BUCKETS[b][1]]
                 nc.sync.dma_start(out=w_raw[:, h * per_head + i:h * per_head + i + n // PASS, 0:PACK],
                                   in_=wdec[h, i * PASS:i * PASS + n].rearrange("(c p j) -> p c j", p=P, j=PACK))
-            v_raw[c] = raw.tile([P, PACK, E], BF16, name="v_raw")
-            nc.sync.dma_start(out=v_raw[c][:], in_=v[h, i * PASS:(i + 1) * PASS, :].rearrange("(p j) e -> p j e", j=PACK))
+            fetch(v, v_raw, "v_raw", c, count)
 
-        def lk(c):
-            h, i, b = chunks[c]
-            k_raw[c] = raw.tile([P, PACK, D], BF16, name="k_raw")
-            nc.sync.dma_start(out=k_raw[c][:], in_=k[h, i * PASS:(i + 1) * PASS, :].rearrange("(p j) d -> p j d", j=PACK))
+        def lk(c, count=1):
+            fetch(k, k_raw, "k_raw", c, count)
 
         def load_q(h):
             q_raw[h] = two.tile([P, TT, D], BF16, name="q_raw")
@@ -215,18 +228,28 @@ def tile_loglinearfenwickbucketread_x1_kernel(tc, q, k, v, wdec, lam, out_0, out
             q_scales[h] = two.tile([P, C], U8, name="q_scales", align_bytes=64)
             nc.vector.quantize_mx(out=q_codes[h][:].bitcast(FP8X4), scales=q_scales[h][:], in_=q_grp[h][:])
 
-        def smm(b, ec):
-            passes = [c for c in range(len(chunks)) if chunks[c][2] == b]
-            s_bank[b, ec] = psum1.tile([P, PACK, P], F32, name="state%d" % ec)
+        def state_pass(b, ec, t, c, passes):
+            if (b, ec) not in s_bank:
+                s_bank[b, ec] = psum1.tile([P, PACK, P], F32, name="state%d" % ec)
+            rows = slice(t * P, (t + 1) * P)
             cols = slice(D + ec * P, D + (ec + 1) * P)
+            nc.tensor.matmul_mx(
+                out=s_bank[b, ec][:, t, :],
+                lhsT=kv_codes[c][:, rows].bitcast(FP8X4), lhsT_scale=kv_scales[c][:, rows],
+                rhs=kv_codes[c + 1][:, cols].bitcast(FP8X4), rhs_scale=kv_scales[c + 1][:, cols],
+                start=(c == passes[0]), stop=(c == passes[-1]))
+
+        def smm(b, ec, begun=False):
+            passes = [c for c in range(len(chunks)) if chunks[c][2] == b]
             for t in range(PACK):
-                rows = slice(t * P, (t + 1) * P)
-                for c in passes:
-                    nc.tensor.matmul_mx(
-                        out=s_bank[b, ec][:, t, :],
-                        lhsT=kv_codes[c][:, rows].bitcast(FP8X4), lhsT_scale=kv_scales[c][:, rows],
-                        rhs=kv_codes[c + 1][:, cols].bitcast(FP8X4), rhs_scale=kv_scales[c + 1][:, cols],
-                        start=(c == passes[0]), stop=(c == passes[-1]))
+                for c in (passes[-1:] if begun and t == 0 else passes):
+                    state_pass(b, ec, t, c, passes)
+
+        def pre(b):
+            passes = [c for c in range(len(chunks)) if chunks[c][2] == b]
+            for ec in range(4):
+                for c in passes[:-1]:
+                    state_pass(b, ec, 0, c, passes)
 
         def sevac(b, ec, eng="S"):
             if b not in s_grp:
@@ -300,8 +323,8 @@ def tile_loglinearfenwickbucketread_x1_kernel(tc, q, k, v, wdec, lam, out_0, out
                 queue.dma_start(out=out_2[0, 4 * quad:4 * quad + 4, :].bitcast(I32),
                                 in_=out_scales[32 * quad:32 * quad + 4, :].bitcast(I32))
 
-        table = {"lv": lv, "lk": lk, "lq": load_q, "ga": gates_a, "gb": gates_b, "gc": gates_c, "mult": mult,
-                 "VP": vint, "KP": kint, "oc": o_c, "qk": qk, "Q": quant, "qv": qv, "qT": q_t, "qe": q_e, "qq": qq, "smm": smm,
+        table = {"lv": lv, "lk": lk, "lv2": lambda c: lv(c, 2), "lk2": lambda c: lk(c, 2), "lq": load_q, "ga": gates_a, "gb": gates_b, "gc": gates_c, "mult": mult,
+                 "VP": vint, "KP": kint, "oc": o_c, "qk": qk, "Q": quant, "qv": qv, "qT": q_t, "qe": q_e, "qq": qq, "smm": smm, "pre": pre, "smr": lambda b, ec: smm(b, ec, True),
                  "se": sevac, "sq": sq, "rmm": rmm, "gate": gated, "oT": o_t, "oe": o_e, "oq": oq}
         for job in jobs:
             table[job[0]](*job[1:])

from contextlib import ExitStack

import concourse.mybir as mybir
from concourse.masks import make_identity

F32 = mybir.dt.float32
BF16 = mybir.dt.bfloat16
U32 = mybir.dt.uint32
I32 = mybir.dt.int32
U8 = mybir.dt.uint8
FP8X4 = mybir.dt.float8_e4m3fn_x4
ALU = mybir.AluOpType
ACT = mybir.ActivationFunctionType

P = 128
PACK = 4
PASS = P * PACK
H, C, D, E = 2, 512, 512, 512
LENS = (2048, 1024, 512)
STARTS = (0, 2048, 3072)
PAST = sum(LENS)
TT = C // P
FLOPS = 2 * H * (PAST * D * E + 3 * C * D * E)

AHEAD = 7
BUCKETS = ((0, 2), (0, 1), (1, 0), (0, 0), (1, 1), (1, 2))


def program():
    chunks = []
    for b, (h, l) in enumerate(BUCKETS):
        for i in range(LENS[l] // PASS):
            chunks.append((h, STARTS[l] // PASS + i, b))
    n = len(chunks)

    def smm(b, parts=range(4)):
        return [("smm", b, ec) for ec in parts]

    def se(b, parts=range(4), eng="S"):
        return [("se", b, ec, eng) for ec in parts]

    def rmm(b, tiles=range(4)):
        return [("rmm", b, tt) for tt in tiles]

    def gate(b, level, tiles=range(4)):
        return [("gate", b, tt, level) + (("S",) if level == 0 else ()) for tt in tiles]

    def qT(h):
        return [("qT", h, 0), ("qT", h, 1)]

    def qe(h):
        return [("qe", h, 0, "S"), ("qe", h, 1, "S")]

    back = (3, 2, 1, 0)
    pairs = (1, 0, 3, 2)
    extra = {
        1: smm(0) + [("gb",)],
        2: se(0, pairs) + qT(0),
        3: [("KP", 4, 2, 4, "S")] + smm(1) + [("gc",)],
        4: qe(0)[::-1] + [("sq", 0)] + qT(1),
        5: se(1, back),
        6: qe(1)[::-1] + [("qq", 0)] + rmm(0),
        7: smm(2),
        8: [("sq", 1)] + gate(0, 0, back),
        9: [("qq", 1)] + se(2, back) + rmm(1, (1, 0)),
        10: [("sq", 2)] + rmm(2, (1, 0)) + [("pre", 3)],
        11: [("smr", 3, ec) for ec in range(4)],
    }
    shared = {4: 2}
    jobs = []
    jobs += [("lv", 0), ("lk", 0), ("lv", 1), ("lk", 1), ("lv", 2), ("lk", 2), ("lv2", 3), ("lk2", 3), ("lq", 0), ("lv2", 5), ("lk2", 5), ("lq", 1)]
    jobs += [("ga",), ("mult", 0)]
    for s in range(n - 1):
        if s in (2, 3, 5):
            c = {2: 7, 3: 9, 5: 11}[s]
            jobs += [("lv2", c), ("lk2", c)]
        if s == 7:
            jobs += [("lv", 13), ("lk", 13)]
        jobs += [("VP", s, 0, 4, "S"), ("KP", s, 0, shared.get(s, 4), "V"), ("mult", s + 1)]
        jobs.append(("Q", s) if s else ("qk", s))
        jobs += extra.get(s, [])
    s = n - 1
    jobs += [("VP", s, 0, 2, "S"), ("KP", s, 0, 4, "V")] + gate(1, 1, (0, 1)) + rmm(1, (3, 2)) + [("Q", s)] + gate(2, 0, (0, 1))
    jobs += se(3) + gate(1, 1, (2, 3)) + rmm(2, (3, 2)) + smm(4) + [("VP", s, 2, 4, "V"), ("sq", 3), ("qv", s)]
    jobs += gate(2, 0, (2, 3)) + rmm(3, (0, 1, 3, 2)) + se(4, pairs) + smm(5, back)
    jobs += gate(3, 2, (0, 1)) + [("sq", 4)] + gate(3, 2, (2, 3)) + [("oc", 0, 0, "S")] + se(5, (2, 3, 0, 1))
    jobs += rmm(4, (0, 1)) + [("oT", 0, 0)] + gate(4, 1, (1, 0)) + rmm(4, (3, 2)) + [("sq", 5)] + gate(4, 1, (2, 3))
    jobs += [("oc", 0, 1, "S"), ("oT", 0, 1), ("oc", 0, 3, "S"), ("oe", 0, 0, "S"), ("oc", 0, 2, "S")]
    jobs += rmm(5, (0, 1)) + gate(5, 2, (0,)) + rmm(5, (3,)) + gate(5, 2, (1,)) + rmm(5, (2,)) + gate(5, 2, (2, 3)) + [("oT", 0, 2), ("oT", 0, 3)]
    jobs += [("oc", 1, tt, "S") for tt in range(3)] + [("oc", 1, 3, "V")]
    jobs += [("oT", 1, tt) for tt in range(4)] + [("oe", 1, 0, "S"), ("oe", 0, 1, "S"), ("oe", 1, 1, "S")]
    jobs += [("oq", 0, 0), ("oq", 1, 0), ("oq", 0, 1), ("oq", 1, 1)]
    return chunks, jobs


def tile_loglinearfenwickbucketread_x1_kernel(tc, q, k, v, wdec, lam, out_0, out_1, out_2):
    nc = tc.nc
    chunks, jobs = program()
    per_head = PAST // PASS

    with ExitStack() as ctx:
        keep = ctx.enter_context(tc.tile_pool(name="keep", bufs=1))
        raw = ctx.enter_context(tc.tile_pool(name="raw", bufs=4))
        mid = ctx.enter_context(tc.tile_pool(name="mid", bufs=4))
        codes = ctx.enter_context(tc.tile_pool(name="codes", bufs=8))
        two = ctx.enter_context(tc.tile_pool(name="two", bufs=2))
        psum1 = ctx.enter_context(tc.psum_pool(name="psum1", bufs=1))
        psum2 = ctx.enter_context(tc.psum_pool(name="psum2", bufs=4))
        states = ctx.enter_context(tc.tile_pool(name="states", bufs=len(BUCKETS)))
        ctx.enter_context(tc.manual_schedule())

        ident = keep.tile([P, P], F32, name="ident")
        make_identity(nc, ident[:])

        w_raw = keep.tile([P, H * per_head, 16], BF16, name="w_raw")
        lam_raw = keep.tile([P, H * 2, 16], BF16, name="lam_raw")
        nc.scalar.dma_start(out=lam_raw[:, :, 0:6], in_=lam.rearrange("h (f p a) l -> p (h f) (a l)", p=P, a=2))
        neg_abs = keep.tile([P, H * 2, 6], F32, name="neg_abs")
        expo = keep.tile([P, H * 2, 6], F32, name="expo")
        logt = keep.tile([P, H * 2, 6], F32, name="logt")
        soft = keep.tile([P, H * 2, 6], F32, name="soft")
        gate = keep.tile([P, H * 2, 6], F32, name="gate")
        out_codes = keep.tile([P, H * C], U32, name="out_codes", align_bytes=64)
        out_scales = keep.tile([P, H * C], U8, name="out_scales", align_bytes=64)

        k_raw, v_raw, v_mul, kv_grp = {}, {}, {}, {}
        kv_codes, kv_scales = {}, {}
        q_raw, q_grp, q_codes, q_scales = {}, {}, {}, {}
        s_bank, s_grp, s_codes, s_scales = {}, {}, {}, {}
        acc, o_grp, banks, o_bf = {}, {}, {}, {}

        def fetch(src, held, name, c, count):
            h, i, b = chunks[c]
            if c == 1:
                slot = held["first"][:, 1:2]
            else:
                pair = raw.tile([P, 2, PACK, D], BF16, name=name)
                held["first"] = pair
                slot = pair[:, 0:count]
            nc.sync.dma_start(out=slot, in_=src[h, i * PASS:(i + count) * PASS, :].rearrange("(g p j) d -> p g j d", p=P, j=PACK))
            for g in range(count):
                held[c + g] = slot[:, g]

        def lv(c, count=1):
            h, i, b = chunks[c]
            if c == 0 or chunks[c - 1][2] != b:
                n = LENS[BUCKETS[b][1]]
                nc.sync.dma_start(out=w_raw[:, h * per_head + i:h * per_head + i + n // PASS, 0:PACK],
                                  in_=wdec[h, i * PASS:i * PASS + n].rearrange("(c p j) -> p c j", p=P, j=PACK))
            fetch(v, v_raw, "v_raw", c, count)

        def lk(c, count=1):
            fetch(k, k_raw, "k_raw", c, count)

        def load_q(h):
            q_raw[h] = two.tile([P, TT, D], BF16, name="q_raw")
            nc.sync.dma_start(out=q_raw[h][:].rearrange("p (f a) d -> p f a d", a=2), in_=q[h].rearrange("(f p a) d -> p f a d", p=P, a=2))

        def gates_a():
            lam_v = lam_raw[:, :, 0:6]
            nc.vector.scalar_tensor_tensor(out=neg_abs[:], in0=lam_v, scalar=-1.0, in1=lam_v, op0=ALU.mult, op1=ALU.min)
            nc.scalar.activation(out=expo[:], in_=neg_abs[:], func=ACT.Exp)
            nc.scalar.activation(out=logt[:], in_=expo[:], func=ACT.Ln, bias=1.0)

        def gates_b():
            nc.vector.scalar_tensor_tensor(out=soft[:], in0=lam_raw[:, :, 0:6], scalar=0.0, in1=logt[:], op0=ALU.max, op1=ALU.add)

        def gates_c():
            nc.vector.tensor_scalar(out=gate[:], in0=soft[:], scalar1=D ** -0.5, scalar2=None, op0=ALU.mult)

        def mult(c):
            h, i, b = chunks[c]
            v_mul[c] = mid.tile([P, PACK, E], BF16, name="v_mul")
            for j in range(PACK):
                nc.vector.tensor_scalar(out=v_mul[c][:, j, :], in0=v_raw[c][:, j, :],
                                        scalar1=w_raw[:, h * per_head + i, j:j + 1], scalar2=None, op0=ALU.mult)

        def copy(eng, out, in_):
            if eng == "S":
                nc.scalar.copy(out=out, in_=in_)
            elif eng == "G":
                nc.gpsimd.tensor_scalar(out=out, in0=in_, scalar1=1.0, scalar2=1.0, op0=ALU.mult, op1=ALU.mult)
            else:
                nc.vector.tensor_copy(out=out, in_=in_)

        def grouped(s):
            if s not in kv_grp:
                kv_grp[s] = mid.tile([P, (D + E) * PACK], BF16, name="kv_grp", align_bytes=64)
            return kv_grp[s]

        def vint(c, lo, hi, eng):
            lo, hi = lo * P, hi * P
            copy(eng, grouped(c + 1)[:, (D + lo) * PACK:(D + hi) * PACK].rearrange("p (e i j) -> p e j i", i=4, j=PACK),
                 v_mul[c][:, :, lo:hi].rearrange("p j (e i) -> p e j i", i=4))

        def kint(c, lo, hi, eng):
            lo, hi = lo * P, hi * P
            dst = grouped(c)[:, 0:D * PACK].rearrange("p (t a b j) -> p a t b j", t=PACK, b=2, j=PACK)
            copy(eng, dst[:, lo // 8:hi // 8], k_raw[c][:, :, lo:hi].rearrange("p j (a b t) -> p a t b j", t=PACK, b=2))

        def quant(s, lo=0, hi=D + E):
            kv_codes[s] = codes.tile([P, D + E], U32, name="kv_codes", align_bytes=64)
            kv_scales[s] = codes.tile([P, D + E], U8, name="kv_scales", align_bytes=64)
            nc.vector.quantize_mx(out=kv_codes[s][:, lo:hi].bitcast(FP8X4), scales=kv_scales[s][:, lo:hi],
                                  in_=kv_grp[s][:, lo * PACK:hi * PACK])

        def qk(c):
            quant(c, 0, D)

        def qv(c):
            quant(c + 1, D, D + E)

        def q_t(h, half):
            banks["q", h, half] = psum2.tile([P, 2, 2, P], F32, name="bank")
            for a in range(2):
                words = q_raw[h][:, 2 * half + a, :].bitcast(F32)
                for u in range(2):
                    nc.tensor.transpose(banks["q", h, half][:, a, u, :], words[:, u:D // 2:2], ident[:])

        def q_e(h, half, eng="S"):
            if h not in q_grp:
                q_grp[h] = two.tile([P, C * PACK], BF16, name="q_grp", align_bytes=64)
            dst = q_grp[h][:].bitcast(F32)[:, half * PASS:(half + 1) * PASS]
            copy(eng, dst.rearrange("p (a r u) -> p a r u", a=2, u=2), banks["q", h, half][:].rearrange("p a u r -> p a r u"))

        def qq(h):
            q_codes[h] = two.tile([P, C], U32, name="q_codes", align_bytes=64)
            q_scales[h] = two.tile([P, C], U8, name="q_scales", align_bytes=64)
            nc.vector.quantize_mx(out=q_codes[h][:].bitcast(FP8X4), scales=q_scales[h][:], in_=q_grp[h][:])

        def state_pass(b, ec, t, c, passes):
            if (b, ec) not in s_bank:
                s_bank[b, ec] = psum1.tile([P, PACK, P], F32, name="state%d" % ec)
            rows = slice(t * P, (t + 1) * P)
            cols = slice(D + ec * P, D + (ec + 1) * P)
            nc.tensor.matmul_mx(
                out=s_bank[b, ec][:, t, :],
                lhsT=kv_codes[c][:, rows].bitcast(FP8X4), lhsT_scale=kv_scales[c][:, rows],
                rhs=kv_codes[c + 1][:, cols].bitcast(FP8X4), rhs_scale=kv_scales[c + 1][:, cols],
                start=(c == passes[0]), stop=(c == passes[-1]))

        def smm(b, ec, begun=False):
            passes = [c for c in range(len(chunks)) if chunks[c][2] == b]
            for t in range(PACK):
                for c in (passes[-1:] if begun and t == 0 else passes):
                    state_pass(b, ec, t, c, passes)

        def pre(b):
            passes = [c for c in range(len(chunks)) if chunks[c][2] == b]
            for ec in range(4):
                for c in passes[:-1]:
                    state_pass(b, ec, 0, c, passes)

        def sevac(b, ec, eng="S"):
            if b not in s_grp:
                s_grp[b] = two.tile([P, E * PACK], BF16, name="s_grp", align_bytes=64)
            dst = s_grp[b][:, ec * PASS:(ec + 1) * PASS].rearrange("p (e t) -> p e t", t=PACK)
            src = s_bank[b, ec][:].rearrange("p t e -> p e t")
            scale = LENS[BUCKETS[b][1]] ** -0.5
            if eng == "S":
                nc.scalar.activation(out=dst, in_=src, func=ACT.Copy, scale=scale)
            else:
                nc.vector.tensor_scalar(out=dst, in0=src, scalar1=scale, scalar2=None, op0=ALU.mult)

        def sq(b):
            s_codes[b] = states.tile([P, E], U32, name="s_codes", align_bytes=64)
            s_scales[b] = states.tile([P, E], U8, name="s_scales", align_bytes=64)
            nc.vector.quantize_mx(out=s_codes[b][:].bitcast(FP8X4), scales=s_scales[b][:], in_=s_grp[b][:])

        def rmm(b, tt):
            h, l = BUCKETS[b]
            banks["r", b, tt] = psum2.tile([P, E], F32, name="bank")
            rows = slice(tt * P, (tt + 1) * P)
            nc.tensor.matmul_mx(
                out=banks["r", b, tt][:],
                lhsT=q_codes[h][:, rows].bitcast(FP8X4), lhsT_scale=q_scales[h][:, rows],
                rhs=s_codes[b][:].bitcast(FP8X4), rhs_scale=s_scales[b][:],
                start=True, stop=True)

        def gated(b, tt, level, eng="V"):
            h, l = BUCKETS[b]
            if h not in acc:
                acc[h] = two.tile([P, TT, E], F32, name="acc")
            bank = banks["r", b, tt]
            g = gate[:, h * 2 + tt // 2, (tt % 2) * 3 + l:(tt % 2) * 3 + l + 1]
            if level == 0 and eng == "S":
                nc.scalar.activation(out=acc[h][:, tt, :], in_=bank[:], func=ACT.Copy, scale=g)
            elif level == 0:
                nc.vector.tensor_scalar(out=acc[h][:, tt, :], in0=bank[:], scalar1=g, scalar2=None, op0=ALU.mult)
            else:
                nc.vector.scalar_tensor_tensor(out=acc[h][:, tt, :], in0=bank[:], scalar=g, in1=acc[h][:, tt, :],
                                               op0=ALU.mult, op1=ALU.add)
            if level == 2:
                nc.sync.dma_start(out=out_0[h].rearrange("(f p a) e -> f a p e", p=P, a=2)[tt // 2, tt % 2], in_=acc[h][:, tt, :])

        def o_c(h, tt, eng):
            o_bf[h, tt] = mid.tile([P, E], BF16, name="o_bf")
            copy(eng, o_bf[h, tt][:].rearrange("p (u r e) -> p u r e", u=2, e=2),
                 acc[h][:, tt, :].rearrange("p (r u e) -> p u r e", u=2, e=2))

        def o_t(h, tt):
            if ("o", h, tt // 2) not in banks:
                banks["o", h, tt // 2] = psum2.tile([P, 2, 2, P], F32, name="bank")
            words = o_bf[h, tt][:].bitcast(F32)
            for u in range(2):
                nc.tensor.transpose(banks["o", h, tt // 2][:, tt % 2, u, :], words[:, u * P:(u + 1) * P], ident[:])

        def o_e(h, half, eng="S"):
            if h not in o_grp:
                o_grp[h] = two.tile([P, C * PACK], BF16, name="o_grp", align_bytes=64)
            dst = o_grp[h][:].bitcast(F32)[:, half * PASS:(half + 1) * PASS]
            copy(eng, dst.rearrange("p (r a u) -> p r a u", a=2, u=2), banks["o", h, half][:].rearrange("p a u r -> p r a u"))

        def oq(h, half):
            cols = slice(h * C + half * C // 2, h * C + (half + 1) * C // 2)
            nc.vector.quantize_mx(out=out_codes[:, cols].bitcast(FP8X4), scales=out_scales[:, cols], in_=o_grp[h][:, half * 2 * C:(half + 1) * 2 * C])
            words = out_1[0].rearrange("p m t -> p (m t)").bitcast(I32)
            nc.sync.dma_start(out=words[:, cols], in_=out_codes[:, cols].bitcast(I32))

        def store_scales():
            for quad in range(4):
                queue = nc.scalar if quad % 2 else nc.sync
                queue.dma_start(out=out_2[0, 4 * quad:4 * quad + 4, :].bitcast(I32),
                                in_=out_scales[32 * quad:32 * quad + 4, :].bitcast(I32))

        table = {"lv": lv, "lk": lk, "lv2": lambda c: lv(c, 2), "lk2": lambda c: lk(c, 2), "lq": load_q, "ga": gates_a, "gb": gates_b, "gc": gates_c, "mult": mult,
                 "VP": vint, "KP": kint, "oc": o_c, "qk": qk, "Q": quant, "qv": qv, "qT": q_t, "qe": q_e, "qq": qq, "smm": smm, "pre": pre, "smr": lambda b, ec: smm(b, ec, True),
                 "se": sevac, "sq": sq, "rmm": rmm, "gate": gated, "oT": o_t, "oe": o_e, "oq": oq}
        for job in jobs:
            table[job[0]](*job[1:])
        store_scales()
